import numpy as np
import ml_dtypes


def mxq(x, axis, fmt="e4m3"):
    dtype, down = {"e4m3": (ml_dtypes.float8_e4m3fn, 7), "e5m2": (ml_dtypes.float8_e5m2, 14)}[fmt]
    v = np.moveaxis(np.asarray(x, np.float32).astype(ml_dtypes.bfloat16).astype(np.float64), axis, -1)
    blocks = v.reshape(v.shape[:-1] + (-1, 32))
    amax = np.abs(blocks).max(-1, keepdims=True)
    byte = np.maximum(np.where(amax > 0, np.frexp(amax)[1] - 1 + 127, 0) - down, 1)
    scale = np.exp2(byte - 127.0)
    codes = (blocks / scale).astype(np.float32).astype(dtype).astype(np.float64)
    return np.moveaxis((codes * scale).reshape(v.shape), -1, axis)


WIDE = False


def mx_kscale(k):
    if not WIDE:
        return np.ones(k)
    levels = np.array([10, -10, 5, -5, 0])
    if k % 512:
        return np.exp2(np.random.permutation(np.resize(levels, k // 32))).repeat(32)
    a = np.empty((k // 512, 16))
    for p in range(k // 512):
        a[p, :8] = np.random.permutation(np.resize(levels, 8))
        for g in range(8):
            far = levels[np.abs(levels - a[p, g]) >= 10]
            a[p, g + 8] = far[np.random.randint(len(far))]
    return np.exp2(a.ravel()).repeat(32)


def f64(x):
    return np.asarray(x).astype(np.float64)


def striped(idx):
    return np.tile(idx.reshape(-1, 16).T, (8, 1)).astype(np.uint16)


def unstriped(offs):
    return offs[:16].T.reshape(-1).astype(np.int64)


def pack_weight(w):
    k, n = w.shape
    w = f64(np.asarray(w, np.float32).astype(ml_dtypes.bfloat16)).reshape(k // 32, 32, n)
    amax = np.abs(w).max(1)
    byte = np.clip(np.where(amax > 0, np.frexp(amax)[1] - 1 + 127 - 7, 1), 1, 254)
    scaled = (w * np.exp2(127.0 - byte)[:, None, :]).reshape(k, n).astype(np.float32)
    words = np.ascontiguousarray(scaled.reshape(k // 512, 128, 4, n).transpose(0, 1, 3, 2)).astype(ml_dtypes.float8_e4m3fn).view(np.uint8)
    return words, np.ascontiguousarray(byte.astype(np.uint8).reshape(k // 512, 16, n))


def unpack_weight(words, scales):
    g, p, n, _ = words.shape
    vals = np.ascontiguousarray(words).view(ml_dtypes.float8_e4m3fn).astype(np.float64) * np.repeat(np.exp2(scales.astype(np.float64) - 127.0), 8, axis=1)[..., None]
    return vals.transpose(0, 1, 3, 2).reshape(g * 512, n)


def relu(v):
    return np.maximum(v, 0.0)


K, T, E, C, N = 512, 1024, 12, 256, 256
TOP = 3
M = 1024


def by_expert(wq, xq):
    return np.concatenate([wq[e].T @ xq[:, e * C:(e + 1) * C] for e in range(E)], axis=1)


def setup_inputs():
    n = np.random.standard_normal
    s = mx_kscale(K)[:, None]
    deal = np.repeat(np.arange(E), C).reshape(TOP, T)[:, np.random.permutation(T)]
    deal = np.take_along_axis(deal, np.argsort(np.random.rand(TOP, T), axis=0), axis=0)
    for _ in range(8):
        s_, t_ = np.random.permutation(T).reshape(2, -1); r = np.random.randint(TOP, size=T // 2); x, y = deal[r, s_].copy(), deal[r, t_].copy()
        ok = ~((deal[:, s_] == y).any(0) | (deal[:, t_] == x).any(0)); deal[r[ok], s_[ok]] = y[ok]; deal[r[ok], t_[ok]] = x[ok]
    order = np.lexsort((np.random.rand(TOP * T), deal.reshape(-1)))
    slot_token = order % T; pos = np.empty(TOP * T, np.int64); pos[order] = np.arange(TOP * T); pos = pos.reshape(TOP, T)
    g = np.random.uniform(0.5, 1.5, (TOP, T)); g = g / g.sum(0)
    packed = [pack_weight(m) for m in n((E, K, N)) / np.sqrt(K) / s[None]]
    r = mx_kscale(M)[:, None]
    return {
        "uT": (n((M, T)) * r).astype(np.float32),
        "wu": (n((M, K)) / np.sqrt(M) / r * s.T).astype(np.float32),
        "w_words": np.stack([m[0] for m in packed]),
        "w_scales": np.stack([m[1] for m in packed]),
        "b": (0.3 * n((N, E))).astype(np.float32),
        "gate": np.stack([np.tile(r, (N, 1)) for r in g]).astype(np.float32),
        "offs": striped(slot_token),
        "pos1": striped(pos[0]),
        "pos2": striped(pos[1]),
        "pos3": striped(pos[2]),
    }


def reference(uT, wu, w_words, w_scales, b, gate, offs, pos1, pos2, pos3):
    idx = unstriped(offs)
    w = np.stack([unpack_weight(w_words[e], w_scales[e]) for e in range(E)])
    x = mxq(f64(wu), 0, "e4m3").T @ mxq(f64(uT), 0, "e4m3")
    xq = mxq(x[:, idx], 0, "e4m3")
    y = by_expert(w, xq)
    y = relu(y + np.repeat(f64(b), C, axis=1))
    return sum(f64(gate[r]) * y[:, unstriped(p)] for r, p in enumerate((pos1, pos2, pos3)))

@@ -1,0 +1,296 @@
+from contextlib import ExitStack
+
+import concourse.mybir as mybir
+from concourse.masks import make_identity
+
+F32 = mybir.dt.float32
+BF16 = mybir.dt.bfloat16
+I32 = mybir.dt.int32
+U32 = mybir.dt.uint32
+U16 = mybir.dt.uint16
+U8 = mybir.dt.uint8
+FP8X4 = mybir.dt.float8_e4m3fn_x4
+ACT = mybir.ActivationFunctionType
+ALU = mybir.AluOpType
+
+P = 128
+F, K, T, E, C, N, TOP = 1024, 512, 1024, 12, 256, 256, 3
+S = E * C
+HALF = T // 2
+FLOPS = 2 * F * K * T + 2 * K * N * S
+BYTES = 4 * F * T + 4 * F * K + E * K * N + E * 16 * N + 4 * N * E + 4 * TOP * T + 2 * P * (S + TOP * T) // 16 + 4 * N * T
+
+TOKEN_PIECES = [(0, 256), (256, 256), (512, 256), (768, 128), (896, 128)]
+SLOT_CHUNKS = [(0, 512), (512, 512), (1024, 512), (1536, 512), (2048, 512), (2560, 256), (2816, 256)]
+
+
+def tile_moe_prv_lin_relu_kernel(
+    tc, uT, wu, w_words, w_scales, b, gate, offs, pos1, pos2, pos3, out
+):
+    nc = tc.nc
+    with ExitStack() as ctx:
+        keep = ctx.enter_context(tc.tile_pool(name="keep", bufs=1))
+        psum = ctx.enter_context(tc.psum_pool(name="psum", bufs=2))
+
+        def bank(tag):
+            return psum.tile([P, 512], F32, name=tag, tag=tag, bufs=4 if tag == "mx" else 2)
+
+        def load_rows(src, g, c0, width, name):
+            raw = keep.tile([P, 4, width], F32, name=name, tag=name)
+            nc.sync.dma_start(out=raw[:], in_=src[g * 512 : (g + 1) * 512, c0 : c0 + width].rearrange("(p j) w -> p j w", j=4))
+            return raw
+
+        w_planes = keep.tile([P, E, N], U8, name="w_planes", align_bytes=64)
+        nc.vector.memset(w_planes[:].bitcast(I32), 0)
+        gate_rows = keep.tile([P, TOP, P], F32, name="gate_rows")
+        nc.vector.memset(gate_rows[:], 0.0)
+        ident = keep.tile([P, P], F32, name="ident")
+        make_identity(nc, ident[:])
+
+        wu_raw = [None, None]
+        u0_raw = [None, None]
+        u1_raw = [None] * len(TOKEN_PIECES)
+        wu_raw[0] = load_rows(wu, 0, 0, K, "wu_raw0")
+        u0_raw[0] = load_rows(uT, 0, 0, HALF, "u0_raw0")
+        wu_raw[1] = load_rows(wu, 1, 0, K, "wu_raw1")
+        u1_raw[0] = load_rows(uT, 1, *TOKEN_PIECES[0], "u1_raw0")
+        u0_raw[1] = load_rows(uT, 0, HALF, HALF, "u0_raw1")
+        for i in range(1, len(TOKEN_PIECES)):
+            u1_raw[i] = load_rows(uT, 1, *TOKEN_PIECES[i], "u1_raw%d" % i)
+
+        offs_t = keep.tile([P, S // 16], U16, name="offs_t")
+        nc.sync.dma_start(offs_t[:], offs)
+        for r in range(4):
+            nc.sync.dma_start(
+                out=w_planes[r:P:32, :, :].bitcast(I32),
+                in_=w_scales[:, 0, r:16:4, :].rearrange("e q n -> q e n").bitcast(I32),
+            )
+        bias = keep.tile([P, 2, E], F32, name="bias")
+        nc.sync.dma_start(out=bias[:], in_=b.rearrange("(c p) e -> p c e", p=P))
+        w_codes = []
+        for i in range(3):
+            wt = keep.tile([P, 4, 4 * N], U8, name="w_codes%d" % i, align_bytes=64)
+            nc.sync.dma_start(
+                out=wt[:].bitcast(I32),
+                in_=w_words[4 * i : 4 * i + 4, 0].rearrange("e p n r -> p e (n r)").bitcast(I32),
+            )
+            w_codes.append(wt)
+        nc.sync.dma_start(out=gate_rows[0:8, :, :], in_=gate[:, 0, :].rearrange("r (c t) -> c r t", t=P))
+        pos_t = []
+        for i, pos in enumerate((pos1, pos2, pos3)):
+            pt = keep.tile([P, T // 16], U16, name="pos_t%d" % i)
+            nc.sync.dma_start(pt[:], pos)
+            pos_t.append(pt)
+        gate_last = keep.tile([P, T], F32, name="gate_last")
+        nc.sync.dma_start(out=gate_last[:], in_=gate[TOP - 1, 0:P, :])
+
+        def quantize(grouped, width, name):
+            codes = keep.tile([P, width], U32, name=name + "_c", tag=name + "_c", align_bytes=64)
+            scales = keep.tile([P, width], U8, name=name + "_s", tag=name + "_s", align_bytes=64)
+            nc.vector.quantize_mx(out=codes[:].bitcast(FP8X4), scales=scales[:], in_=grouped)
+            return codes, scales
+
+        def prep_wu(g):
+            grouped = keep.tile([P, 4 * K], BF16, name="wu_bf%d" % g, align_bytes=64)
+            dst = grouped[:].rearrange("p (t m j) -> p m t j", t=4, j=4)
+            src = wu_raw[g][:].rearrange("p j (m t) -> p m t j", t=4)
+            cut = 80
+            nc.vector.tensor_copy(out=dst[:, 0:cut], in_=src[:, 0:cut])
+            nc.scalar.activation(out=dst[:, cut:P], in_=src[:, cut:P], func=ACT.Copy)
+            return quantize(grouped[:], K, "wu_q%d" % g)
+
+        def cast_u(raw, c0, width, on_vector, name):
+            grouped = keep.tile([P, 4 * width], BF16, name=name + "_bf", align_bytes=64)
+            dst = grouped[:].rearrange("p (c i j) -> p c j i", i=4, j=4)
+            src = raw[:, :, c0 : c0 + width].rearrange("p j (c i) -> p c j i", i=4)
+            if on_vector:
+                nc.vector.tensor_copy(out=dst, in_=src)
+            else:
+                nc.scalar.activation(out=dst, in_=src, func=ACT.Copy)
+            return grouped[:]
+
+
+        def project(i, u, on_vector):
+            t0, width = TOKEN_PIECES[i]
+            acc = bank("mx" if u == 0 else ("turned" if i % 2 else "summed"))
+            first = u0_q[t0 // 256]
+            c0 = t0 % 256
+            for e in range(2):
+                cols = slice((2 * u + e) * P, (2 * u + e + 1) * P)
+                for g in range(2):
+                    codes, scales = (first[0][:, c0 : c0 + width], first[1][:, c0 : c0 + width]) if g == 0 else (u1_q[i][0][:], u1_q[i][1][:])
+                    nc.tensor.matmul_mx(
+                        out=acc[:, e * width : (e + 1) * width],
+                        lhsT=wu_q[g][0][:, cols].bitcast(FP8X4),
+                        lhsT_scale=wu_q[g][1][:, cols],
+                        rhs=codes.bitcast(FP8X4),
+                        rhs_scale=scales,
+                        start=(g == 0),
+                        stop=(g == 1),
+                    )
+            dst = x_pairs[u][:, t0 : t0 + width].bitcast(BF16).rearrange("p (t e) -> p t e", e=2)
+            src = acc[:, 0 : 2 * width].rearrange("p (e t) -> p t e", e=2)
+            if on_vector:
+                nc.vector.tensor_copy(out=dst, in_=src)
+            else:
+                nc.scalar.copy(out=dst, in_=src)
+
+        wu_q = [None, None]
+        u0_q = [None] * 4
+        u1_q = [None] * len(TOKEN_PIECES)
+        wu_q[0] = prep_wu(0)
+        bf_a = cast_u(u0_raw[0], 0, 256, True, "u0a")
+        bf_b = cast_u(u0_raw[0], 256, 256, False, "u0b")
+        u0_q[0] = quantize(bf_a, 256, "u0_q0")
+        u0_q[1] = quantize(bf_b, 256, "u0_q1")
+        wu_q[1] = prep_wu(1)
+        u1_q[0] = quantize(cast_u(u1_raw[0], 0, 256, True, "u1a"), 256, "u1_q0")
+        bf_a = cast_u(u0_raw[1], 0, 256, True, "u0c")
+        bf_b = cast_u(u0_raw[1], 256, 256, False, "u0d")
+        x_pairs = [
+            keep.tile([P, T], U32, name="x_pairs0", tag="u0_raw1"),
+            keep.tile([P, T], U32, name="x_pairs1"),
+        ]
+        project(0, 0, False)
+        project(0, 1, False)
+        u0_q[2] = quantize(bf_a, 256, "u0_q2")
+        bf_a = cast_u(u1_raw[1], 0, 256, True, "u1b")
+        u0_q[3] = quantize(bf_b, 256, "u0_q3")
+        u1_q[1] = quantize(bf_a, 256, "u1_q1")
+        project(1, 0, False)
+        bf_a = cast_u(u1_raw[2], 0, 256, True, "u1c")
+        bf_b = cast_u(u1_raw[3], 0, 128, True, "u1d")
+        project(1, 1, False)
+        u1_q[2] = quantize(bf_a, 256, "u1_q2")
+        bf_a = cast_u(u1_raw[4], 0, 128, True, "u1e")
+        u1_q[3] = quantize(bf_b, 128, "u1_q3")
+        u1_q[4] = quantize(bf_a, 128, "u1_q4")
+        project(2, 0, False)
+        project(3, 0, True)
+        project(4, 0, True)
+        project(2, 1, False)
+        project(3, 1, False)
+        project(4, 1, False)
+
+        y = [keep.tile([P, S], F32, name="y%d" % nb) for nb in range(2)]
+        last = len(SLOT_CHUNKS) - 1
+        stage = [keep.tile([P, 1024], U32, name="stage%d" % i, align_bytes=64) for i in range(3)]
+
+        def picked(n):
+            return stage[n % 3][:, 0 : 2 * SLOT_CHUNKS[n][1]]
+
+        def woven(n):
+            return stage[(n + 2) % 3][:, 0 : 2 * SLOT_CHUNKS[n][1]]
+
+        def gather(n, u):
+            s0, width = SLOT_CHUNKS[n]
+            lst = offs_t[:, s0 // 16 : (s0 + width) // 16]
+            if n == last:
+                dst = picked(n).rearrange("p (s u) -> p s u", u=2)[:, :, u]
+            else:
+                dst = picked(n)[:, u * width : (u + 1) * width]
+            nc.vector.tensor_copy(dst, x_pairs[u][:].indirect(lst))
+
+        def weave(n):
+            nc.scalar.copy(
+                out=woven(n).rearrange("p (s u) -> p s u", u=2),
+                in_=picked(n).rearrange("p (u s) -> p s u", u=2),
+            )
+
+        def experts(n, xq, nb):
+            s0, width = SLOT_CHUNKS[n]
+            acc = bank("mx")
+            for i in range(width // C):
+                e = s0 // C + i
+                nc.tensor.matmul_mx(
+                    out=acc[:, i * C : (i + 1) * C],
+                    lhsT=w_codes[e // 4][:, e % 4, nb * 4 * P : (nb + 1) * 4 * P].bitcast(FP8X4),
+                    lhsT_scale=w_planes[:, e, nb * P : (nb + 1) * P],
+                    rhs=xq[0][:, i * C : (i + 1) * C].bitcast(FP8X4),
+                    rhs_scale=xq[1][:, i * C : (i + 1) * C],
+                    start=True,
+                    stop=True,
+                )
+            for i in range(width // C):
+                e = s0 // C + i
+                dst = y[nb][:, e * C : (e + 1) * C]
+                if n == last and nb == 0:
+                    nc.vector.tensor_scalar(dst, acc[:, i * C : (i + 1) * C], bias[:, nb, e : e + 1], 0.0, ALU.add, ALU.max)
+                else:
+                    nc.scalar.activation(out=dst, in_=acc[:, i * C : (i + 1) * C], func=ACT.Relu, bias=bias[:, nb, e : e + 1])
+
+        gate_cols = keep.tile([P, TOP, 8], F32, name="gate_cols")
+
+        def turn_gate():
+            acc = bank("turned")
+            for r in range(TOP):
+                nc.tensor.transpose(acc[:, r * P : (r + 1) * P], gate_rows[:, r, :], ident[:])
+            nc.scalar.copy(out=gate_cols[:], in_=acc[:, 0 : TOP * P].rearrange("p (r c) -> p r c", r=TOP)[:, :, 0:8])
+
+        xq = [None] * len(SLOT_CHUNKS)
+        for u in range(2):
+            for n in range(2):
+                gather(n, u)
+        weave(0)
+        for n in range(last - 1):
+            xq[n] = quantize(woven(n).bitcast(BF16), SLOT_CHUNKS[n][1], "xq")
+            weave(n + 1)
+            gather(n + 2, 0)
+            gather(n + 2, 1)
+            experts(n, xq[n], 0)
+            experts(n, xq[n], 1)
+            if n == 1:
+                turn_gate()
+        for n in (last - 1, last):
+            xq[n] = quantize((picked(n) if n == last else woven(n)).bitcast(BF16), SLOT_CHUNKS[n][1], "xq_last" if n == last else "xq")
+        for nb in range(2):
+            for n in (last - 1, last):
+                experts(n, xq[n], nb)
+
+        def scaled_turned(nb, h, r):
+            got = keep.tile([P, HALF], F32, name="got%d%d%d" % (nb, h, r))
+            nc.vector.tensor_copy(got[:], y[nb][:].indirect(pos_t[r][:, h * 32 : (h + 1) * 32]))
+            acc = bank("turned")
+            for c in range(4):
+                nc.tensor.transpose(acc[:, c * P : (c + 1) * P], got[:, c * P : (c + 1) * P], ident[:])
+            scaled = keep.tile([P, HALF], F32, name="scaled%d%d%d" % (nb, h, r))
+            for c in range(4):
+                nc.scalar.activation(
+                    out=scaled[:, c * P : (c + 1) * P],
+                    in_=acc[:, c * P : (c + 1) * P],
+                    func=ACT.Copy,
+                    scale=gate_cols[:, r, 4 * h + c : 4 * h + c + 1],
+                )
+            return scaled
+
+        def sum_back(terms):
+            acc = bank("summed")
+            for c in range(4):
+                for r, term in enumerate(terms):
+                    nc.tensor.matmul(
+                        acc[:, c * P : (c + 1) * P],
+                        term[:, c * P : (c + 1) * P],
+                        ident[:],
+                        start=(r == 0),
+                        stop=(r == len(terms) - 1),
+                        is_transpose=True,
+                    )
+            return acc
+
+        for h in range(2):
+            acc = sum_back([scaled_turned(0, h, r) for r in range(TOP)])
+            res = keep.tile([P, HALF], F32, name="res0%d" % h)
+            nc.scalar.copy(out=res[:], in_=acc[:])
+            nc.sync.dma_start(out=out[0:P, h * HALF : (h + 1) * HALF], in_=res[:])
+        sums = [sum_back([scaled_turned(1, h, r) for r in range(TOP - 1)]) for h in range(2)]
+        third = []
+        for h in range(2):
+            z = keep.tile([P, HALF], F32, name="third%d" % h)
+            nc.vector.tensor_tensor(
+                z[:], y[1][:].indirect(pos_t[TOP - 1][:, h * 32 : (h + 1) * 32]), gate_last[:, h * HALF : (h + 1) * HALF], ALU.mult
+            )
+            third.append(z)
+        for h in range(2):
+            res = keep.tile([P, HALF], F32, name="res1%d" % h)
+            nc.vector.tensor_tensor(res[:], sums[h][:], third[h][:], ALU.add)
+            nc.sync.dma_start(out=out[P : 2 * P, h * HALF : (h + 1) * HALF], in_=res[:])

@@ -30,10 +30,10 @@ def tile_moe_prv_lin_relu_kernel(
     nc = tc.nc
     with ExitStack() as ctx:
         keep = ctx.enter_context(tc.tile_pool(name="keep", bufs=1))
-        psum = ctx.enter_context(tc.psum_pool(name="psum", bufs=2))
+        psum = ctx.enter_context(tc.psum_pool(name="psum", bufs=1))
 
-        def bank(tag):
-            return psum.tile([P, 512], F32, name=tag, tag=tag, bufs=4 if tag == "mx" else 2)
+        def bank(i):
+            return psum.tile([P, 512], F32, name="bank%d" % i, tag="bank%d" % i)
 
         def load_rows(src, g, c0, width, name):
             raw = keep.tile([P, 4, width], F32, name=name, tag=name)
@@ -81,8 +81,8 @@ def tile_moe_prv_lin_relu_kernel(
             pt = keep.tile([P, T // 16], U16, name="pos_t%d" % i)
             nc.sync.dma_start(pt[:], pos)
             pos_t.append(pt)
-        gate_last = keep.tile([P, T], F32, name="gate_last")
-        nc.sync.dma_start(out=gate_last[:], in_=gate[TOP - 1, 0:P, :])
+        gate_last = keep.tile([P, TOP, HALF], F32, name="gate_last")
+        nc.sync.dma_start(out=gate_last[:], in_=gate[:, 0:P, HALF:T].rearrange("r p t -> p r t"))
 
         def quantize(grouped, width, name):
             codes = keep.tile([P, width], U32, name=name + "_c", tag=name + "_c", align_bytes=64)
@@ -110,9 +110,9 @@ def tile_moe_prv_lin_relu_kernel(
             return grouped[:]
 
 
-        def project(i, u, on_vector):
+        def project(i, u, on_vector, nbank):
             t0, width = TOKEN_PIECES[i]
-            acc = bank("mx" if u == 0 else ("turned" if i % 2 else "summed"))
+            acc = bank(nbank)
             first = u0_q[t0 // 256]
             c0 = t0 % 256
             for e in range(2):
@@ -151,55 +151,52 @@ def tile_moe_prv_lin_relu_kernel(
             keep.tile([P, T], U32, name="x_pairs0", tag="u0_raw1"),
             keep.tile([P, T], U32, name="x_pairs1"),
         ]
-        project(0, 0, False)
-        project(0, 1, False)
+        project(0, 0, False, 0)
+        project(0, 1, False, 1)
         u0_q[2] = quantize(bf_a, 256, "u0_q2")
         bf_a = cast_u(u1_raw[1], 0, 256, True, "u1b")
         u0_q[3] = quantize(bf_b, 256, "u0_q3")
         u1_q[1] = quantize(bf_a, 256, "u1_q1")
-        project(1, 0, False)
+        project(1, 0, False, 2)
         bf_a = cast_u(u1_raw[2], 0, 256, True, "u1c")
         bf_b = cast_u(u1_raw[3], 0, 128, True, "u1d")
-        project(1, 1, False)
+        project(1, 1, False, 3)
         u1_q[2] = quantize(bf_a, 256, "u1_q2")
         bf_a = cast_u(u1_raw[4], 0, 128, True, "u1e")
         u1_q[3] = quantize(bf_b, 128, "u1_q3")
         u1_q[4] = quantize(bf_a, 128, "u1_q4")
-        project(2, 0, False)
-        project(3, 0, True)
-        project(4, 0, True)
-        project(2, 1, False)
-        project(3, 1, False)
-        project(4, 1, False)
+        project(2, 0, False, 4)
+        project(3, 0, True, 5)
+        project(4, 0, True, 6)
+        project(2, 1, False, 7)
+        project(3, 1, False, 0)
+        project(4, 1, False, 1)
 
         y = [keep.tile([P, S], F32, name="y%d" % nb) for nb in range(2)]
-        last = len(SLOT_CHUNKS) - 1
         stage = [keep.tile([P, 1024], U32, name="stage%d" % i, align_bytes=64) for i in range(3)]
 
-        def picked(n):
-            return stage[n % 3][:, 0 : 2 * SLOT_CHUNKS[n][1]]
-
-        def woven(n):
-            return stage[(n + 2) % 3][:, 0 : 2 * SLOT_CHUNKS[n][1]]
+        def staged(n, shift):
+            s0, width = SLOT_CHUNKS[n]
+            c0 = 2 * (s0 % 512)
+            return stage[(s0 // 512 + shift) % 3][:, c0 : c0 + 2 * width]
 
         def gather(n, u):
             s0, width = SLOT_CHUNKS[n]
             lst = offs_t[:, s0 // 16 : (s0 + width) // 16]
-            if n == last:
-                dst = picked(n).rearrange("p (s u) -> p s u", u=2)[:, :, u]
-            else:
-                dst = picked(n)[:, u * width : (u + 1) * width]
-            nc.vector.tensor_copy(dst, x_pairs[u][:].indirect(lst))
+            nc.vector.tensor_copy(staged(n, 0)[:, u * width : (u + 1) * width], x_pairs[u][:].indirect(lst))
 
         def weave(n):
             nc.scalar.copy(
-                out=woven(n).rearrange("p (s u) -> p s u", u=2),
-                in_=picked(n).rearrange("p (u s) -> p s u", u=2),
+                out=staged(n, 2).rearrange("p (s u) -> p s u", u=2),
+                in_=staged(n, 0).rearrange("p (u s) -> p s u", u=2),
             )
 
-        def experts(n, xq, nb):
+        def quantize_slots(n, name):
+            return quantize(staged(n, 2).bitcast(BF16), SLOT_CHUNKS[n][1], name)
+
+        def multiply(n, xq, nb, nbank):
             s0, width = SLOT_CHUNKS[n]
-            acc = bank("mx")
+            acc = bank(nbank)
             for i in range(width // C):
                 e = s0 // C + i
                 nc.tensor.matmul_mx(
@@ -211,10 +208,14 @@ def tile_moe_prv_lin_relu_kernel(
                     start=True,
                     stop=True,
                 )
+            return acc
+
+        def bias_relu(n, nb, acc, on_vector):
+            s0, width = SLOT_CHUNKS[n]
             for i in range(width // C):
                 e = s0 // C + i
                 dst = y[nb][:, e * C : (e + 1) * C]
-                if n == last and nb == 0:
+                if on_vector:
                     nc.vector.tensor_scalar(dst, acc[:, i * C : (i + 1) * C], bias[:, nb, e : e + 1], 0.0, ALU.add, ALU.max)
                 else:
                     nc.scalar.activation(out=dst, in_=acc[:, i * C : (i + 1) * C], func=ACT.Relu, bias=bias[:, nb, e : e + 1])
@@ -222,35 +223,47 @@ def tile_moe_prv_lin_relu_kernel(
         gate_cols = keep.tile([P, TOP, 8], F32, name="gate_cols")
 
         def turn_gate():
-            acc = bank("turned")
+            acc = bank(6)
             for r in range(TOP):
                 nc.tensor.transpose(acc[:, r * P : (r + 1) * P], gate_rows[:, r, :], ident[:])
             nc.scalar.copy(out=gate_cols[:], in_=acc[:, 0 : TOP * P].rearrange("p (r c) -> p r c", r=TOP)[:, :, 0:8])
 
-        xq = [None] * len(SLOT_CHUNKS)
-        for u in range(2):
-            for n in range(2):
+        for n in range(2):
+            for u in range(2):
                 gather(n, u)
         weave(0)
-        for n in range(last - 1):
-            xq[n] = quantize(woven(n).bitcast(BF16), SLOT_CHUNKS[n][1], "xq")
+        for n in range(3):
+            xq = quantize_slots(n, "xq")
             weave(n + 1)
             gather(n + 2, 0)
             gather(n + 2, 1)
-            experts(n, xq[n], 0)
-            experts(n, xq[n], 1)
+            for nb in range(2):
+                bias_relu(n, nb, multiply(n, xq, nb, 2 + 2 * (n % 2) + nb), False)
             if n == 1:
                 turn_gate()
-        for n in (last - 1, last):
-            xq[n] = quantize((picked(n) if n == last else woven(n)).bitcast(BF16), SLOT_CHUNKS[n][1], "xq_last" if n == last else "xq")
-        for nb in range(2):
-            for n in (last - 1, last):
-                experts(n, xq[n], nb)
+        xq = quantize_slots(3, "xq")
+        weave(4)
+        for n in (5, 6):
+            gather(n, 0)
+            gather(n, 1)
+        late = []
+        first_rows = multiply(3, xq, 0, 4)
+        late.append((3, multiply(3, xq, 1, 5)))
+        bias_relu(3, 0, first_rows, False)
+        weave(5)
+        weave(6)
+        tail = [quantize_slots(4, "xq"), quantize_slots(5, "xq5"), quantize_slots(6, "xq6")]
+        for n, nbank in ((4, 2), (5, 6), (6, 7)):
+            bias_relu(n, 0, multiply(n, tail[n - 4], 0, nbank), n > 4)
+        for n, nbank in ((4, 3), (5, 0), (6, 1)):
+            late.append((n, multiply(n, tail[n - 4], 1, nbank)))
+        for n, acc in late:
+            bias_relu(n, 1, acc, False)
 
         def scaled_turned(nb, h, r):
             got = keep.tile([P, HALF], F32, name="got%d%d%d" % (nb, h, r))
             nc.vector.tensor_copy(got[:], y[nb][:].indirect(pos_t[r][:, h * 32 : (h + 1) * 32]))
-            acc = bank("turned")
+            acc = bank((6, 7, 2)[r])
             for c in range(4):
                 nc.tensor.transpose(acc[:, c * P : (c + 1) * P], got[:, c * P : (c + 1) * P], ident[:])
             scaled = keep.tile([P, HALF], F32, name="scaled%d%d%d" % (nb, h, r))
@@ -263,8 +276,8 @@ def tile_moe_prv_lin_relu_kernel(
                 )
             return scaled
 
-        def sum_back(terms):
-            acc = bank("summed")
+        def sum_back(terms, nbank):
+            acc = bank(nbank)
             for c in range(4):
                 for r, term in enumerate(terms):
                     nc.tensor.matmul(
@@ -277,20 +290,22 @@ def tile_moe_prv_lin_relu_kernel(
                     )
             return acc
 
-        for h in range(2):
-            acc = sum_back([scaled_turned(0, h, r) for r in range(TOP)])
-            res = keep.tile([P, HALF], F32, name="res0%d" % h)
+        for i, (nb, h) in enumerate(((0, 0), (0, 1), (1, 0))):
+            acc = sum_back([scaled_turned(nb, h, r) for r in range(TOP)], 4 + i % 2)
+            res = keep.tile([P, HALF], F32, name="res%d%d" % (nb, h))
             nc.scalar.copy(out=res[:], in_=acc[:])
-            nc.sync.dma_start(out=out[0:P, h * HALF : (h + 1) * HALF], in_=res[:])
-        sums = [sum_back([scaled_turned(1, h, r) for r in range(TOP - 1)]) for h in range(2)]
-        third = []
-        for h in range(2):
-            z = keep.tile([P, HALF], F32, name="third%d" % h)
-            nc.vector.tensor_tensor(
-                z[:], y[1][:].indirect(pos_t[TOP - 1][:, h * 32 : (h + 1) * 32]), gate_last[:, h * HALF : (h + 1) * HALF], ALU.mult
-            )
-            third.append(z)
-        for h in range(2):
-            res = keep.tile([P, HALF], F32, name="res1%d" % h)
-            nc.vector.tensor_tensor(res[:], sums[h][:], third[h][:], ALU.add)
-            nc.sync.dma_start(out=out[P : 2 * P, h * HALF : (h + 1) * HALF], in_=res[:])
+            nc.scalar.dma_start(out=out[nb * P : (nb + 1) * P, h * HALF : (h + 1) * HALF], in_=res[:])
+        for q in range(2):
+            t0 = HALF + q * 256
+            terms = []
+            for r in range(TOP):
+                z = keep.tile([P, 256], F32, name="term%d%d" % (q, r))
+                nc.vector.tensor_tensor(
+                    z[:], y[1][:].indirect(pos_t[r][:, t0 // 16 : (t0 + 256) // 16]), gate_last[:, r, q * 256 : (q + 1) * 256], ALU.mult
+                )
+                terms.append(z)
+            part = keep.tile([P, 256], F32, name="part%d" % q)
+            nc.vector.tensor_tensor(part[:], terms[0][:], terms[1][:], ALU.add)
+            res = keep.tile([P, 256], F32, name="last%d" % q)
+            nc.vector.tensor_tensor(res[:], part[:], terms[2][:], ALU.add)
+            nc.sync.dma_start(out=out[P : 2 * P, t0 : t0 + 256], in_=res[:])

@@ -21,7 +21,7 @@ FLOPS = 2 * F * K * T + 2 * K * N * S
 BYTES = 4 * F * T + 4 * F * K + E * K * N + E * 16 * N + 4 * N * E + 4 * TOP * T + 2 * P * (S + TOP * T) // 16 + 4 * N * T
 
 TOKEN_PIECES = [(0, 256), (256, 256), (512, 256), (768, 128), (896, 128)]
-SLOT_CHUNKS = [(0, 512), (512, 512), (1024, 512), (1536, 512), (2048, 512), (2560, 256), (2816, 256)]
+SLOT_CHUNKS = [(0, 256), (256, 512), (768, 512), (1280, 512), (1792, 512), (2304, 512), (2816, 256)]
 
 
 def tile_moe_prv_lin_relu_kernel(
@@ -53,9 +53,9 @@ def tile_moe_prv_lin_relu_kernel(
         wu_raw[0] = load_rows(wu, 0, 0, K, "wu_raw0")
         u0_raw[0] = load_rows(uT, 0, 0, HALF, "u0_raw0")
         wu_raw[1] = load_rows(wu, 1, 0, K, "wu_raw1")
-        u1_raw[0] = load_rows(uT, 1, *TOKEN_PIECES[0], "u1_raw0")
+        u1_raw[0] = load_rows(uT, 1, 0, HALF, "u1_raw0")
         u0_raw[1] = load_rows(uT, 0, HALF, HALF, "u0_raw1")
-        for i in range(1, len(TOKEN_PIECES)):
+        for i in range(2, len(TOKEN_PIECES)):
             u1_raw[i] = load_rows(uT, 1, *TOKEN_PIECES[i], "u1_raw%d" % i)
 
         offs_t = keep.tile([P, S // 16], U16, name="offs_t")
@@ -144,7 +144,10 @@ def tile_moe_prv_lin_relu_kernel(
         u0_q[0] = quantize(bf_a, 256, "u0_q0")
         u0_q[1] = quantize(bf_b, 256, "u0_q1")
         wu_q[1] = prep_wu(1)
-        u1_q[0] = quantize(cast_u(u1_raw[0], 0, 256, True, "u1a"), 256, "u1_q0")
+        bf_a = cast_u(u1_raw[0], 0, 256, True, "u1a")
+        bf_b = cast_u(u1_raw[0], 256, 256, False, "u1b")
+        u1_q[0] = quantize(bf_a, 256, "u1_q0")
+        u1_q[1] = quantize(bf_b, 256, "u1_q1")
         bf_a = cast_u(u0_raw[1], 0, 256, True, "u0c")
         bf_b = cast_u(u0_raw[1], 256, 256, False, "u0d")
         x_pairs = [
@@ -152,15 +155,13 @@ def tile_moe_prv_lin_relu_kernel(
             keep.tile([P, T], U32, name="x_pairs1"),
         ]
         project(0, 0, False, 0)
-        project(0, 1, False, 1)
-        u0_q[2] = quantize(bf_a, 256, "u0_q2")
-        bf_a = cast_u(u1_raw[1], 0, 256, True, "u1b")
-        u0_q[3] = quantize(bf_b, 256, "u0_q3")
-        u1_q[1] = quantize(bf_a, 256, "u1_q1")
         project(1, 0, False, 2)
-        bf_a = cast_u(u1_raw[2], 0, 256, True, "u1c")
-        bf_b = cast_u(u1_raw[3], 0, 128, True, "u1d")
+        project(0, 1, False, 1)
         project(1, 1, False, 3)
+        u0_q[2] = quantize(bf_a, 256, "u0_q2")
+        bf_a = cast_u(u1_raw[2], 0, 256, True, "u1c")
+        u0_q[3] = quantize(bf_b, 256, "u0_q3")
+        bf_b = cast_u(u1_raw[3], 0, 128, True, "u1d")
         u1_q[2] = quantize(bf_a, 256, "u1_q2")
         bf_a = cast_u(u1_raw[4], 0, 128, True, "u1e")
         u1_q[3] = quantize(bf_b, 128, "u1_q3")
@@ -175,24 +176,26 @@ def tile_moe_prv_lin_relu_kernel(
         y = [keep.tile([P, S], F32, name="y%d" % nb) for nb in range(2)]
         stage = [keep.tile([P, 1024], U32, name="stage%d" % i, align_bytes=64) for i in range(3)]
 
-        def staged(n, shift):
-            s0, width = SLOT_CHUNKS[n]
-            c0 = 2 * (s0 % 512)
-            return stage[(s0 // 512 + shift) % 3][:, c0 : c0 + 2 * width]
-
-        def gather(n, u):
-            s0, width = SLOT_CHUNKS[n]
+        def gather(n, c0, width):
+            s0 = SLOT_CHUNKS[n][0] + c0
             lst = offs_t[:, s0 // 16 : (s0 + width) // 16]
-            nc.vector.tensor_copy(staged(n, 0)[:, u * width : (u + 1) * width], x_pairs[u][:].indirect(lst))
+            for u in range(2):
+                d0 = 2 * c0 + u * width
+                nc.vector.tensor_copy(stage[n % 3][:, d0 : d0 + width], x_pairs[u][:].indirect(lst))
 
-        def weave(n):
+        def weave(n, c0, width):
+            cols = slice(2 * c0, 2 * (c0 + width))
             nc.scalar.copy(
-                out=staged(n, 2).rearrange("p (s u) -> p s u", u=2),
-                in_=staged(n, 0).rearrange("p (u s) -> p s u", u=2),
+                out=stage[(n + 2) % 3][:, cols].rearrange("p (s u) -> p s u", u=2),
+                in_=stage[n % 3][:, cols].rearrange("p (u s) -> p s u", u=2),
             )
 
         def quantize_slots(n, name):
-            return quantize(staged(n, 2).bitcast(BF16), SLOT_CHUNKS[n][1], name)
+            woven = stage[(n + 2) % 3]
+            return [
+                quantize(woven[:, 2 * C * i : 2 * C * (i + 1)].bitcast(BF16), C, name + str(i))
+                for i in range(SLOT_CHUNKS[n][1] // C)
+            ]
 
         def multiply(n, xq, nb, nbank):
             s0, width = SLOT_CHUNKS[n]
@@ -203,8 +206,8 @@ def tile_moe_prv_lin_relu_kernel(
                     out=acc[:, i * C : (i + 1) * C],
                     lhsT=w_codes[e // 4][:, e % 4, nb * 4 * P : (nb + 1) * 4 * P].bitcast(FP8X4),
                     lhsT_scale=w_planes[:, e, nb * P : (nb + 1) * P],
-                    rhs=xq[0][:, i * C : (i + 1) * C].bitcast(FP8X4),
-                    rhs_scale=xq[1][:, i * C : (i + 1) * C],
+                    rhs=xq[i][0][:].bitcast(FP8X4),
+                    rhs_scale=xq[i][1][:],
                     start=True,
                     stop=True,
                 )
@@ -228,42 +231,38 @@ def tile_moe_prv_lin_relu_kernel(
                 nc.tensor.transpose(acc[:, r * P : (r + 1) * P], gate_rows[:, r, :], ident[:])
             nc.scalar.copy(out=gate_cols[:], in_=acc[:, 0 : TOP * P].rearrange("p (r c) -> p r c", r=TOP)[:, :, 0:8])
 
-        for n in range(2):
-            for u in range(2):
-                gather(n, u)
-        weave(0)
-        for n in range(3):
+        gather(0, 0, 256)
+        gather(1, 0, 512)
+        weave(0, 0, 256)
+        for n in range(4):
             xq = quantize_slots(n, "xq")
-            weave(n + 1)
-            gather(n + 2, 0)
-            gather(n + 2, 1)
+            weave(n + 1, 0, 512)
+            gather(n + 2, 0, 512)
             for nb in range(2):
                 bias_relu(n, nb, multiply(n, xq, nb, 2 + 2 * (n % 2) + nb), False)
             if n == 1:
                 turn_gate()
-        xq = quantize_slots(3, "xq")
-        weave(4)
-        for n in (5, 6):
-            gather(n, 0)
-            gather(n, 1)
-        late = []
-        first_rows = multiply(3, xq, 0, 4)
-        late.append((3, multiply(3, xq, 1, 5)))
-        bias_relu(3, 0, first_rows, False)
-        weave(5)
-        weave(6)
-        tail = [quantize_slots(4, "xq"), quantize_slots(5, "xq5"), quantize_slots(6, "xq6")]
-        for n, nbank in ((4, 2), (5, 6), (6, 7)):
-            bias_relu(n, 0, multiply(n, tail[n - 4], 0, nbank), n > 4)
-        for n, nbank in ((4, 3), (5, 0), (6, 1)):
-            late.append((n, multiply(n, tail[n - 4], 1, nbank)))
+        xq = quantize_slots(4, "xq")
+        weave(5, 0, 512)
+        gather(6, 0, 128)
+        gather(6, 128, 128)
+        weave(6, 0, 128)
+        weave(6, 128, 128)
+        first_rows = multiply(4, xq, 0, 2)
+        late = [(4, multiply(4, xq, 1, 3))]
+        bias_relu(4, 0, first_rows, False)
+        tail = [quantize_slots(5, "xq5_"), quantize_slots(6, "xq6_")]
+        for n, nbank in ((5, 4), (6, 6)):
+            bias_relu(n, 0, multiply(n, tail[n - 5], 0, nbank), n == 6)
+        for n, nbank in ((5, 6), (6, 0)):
+            late.append((n, multiply(n, tail[n - 5], 1, nbank)))
         for n, acc in late:
             bias_relu(n, 1, acc, False)
 
-        def scaled_turned(nb, h, r):
+        def scaled_turned(nb, h, r, nbank):
             got = keep.tile([P, HALF], F32, name="got%d%d%d" % (nb, h, r))
             nc.vector.tensor_copy(got[:], y[nb][:].indirect(pos_t[r][:, h * 32 : (h + 1) * 32]))
-            acc = bank((6, 7, 2)[r])
+            acc = bank(nbank)
             for c in range(4):
                 nc.tensor.transpose(acc[:, c * P : (c + 1) * P], got[:, c * P : (c + 1) * P], ident[:])
             scaled = keep.tile([P, HALF], F32, name="scaled%d%d%d" % (nb, h, r))
@@ -276,36 +275,47 @@ def tile_moe_prv_lin_relu_kernel(
                 )
             return scaled
 
-        def sum_back(terms, nbank):
+        def sum_back(terms, nbank, blocks, res):
             acc = bank(nbank)
-            for c in range(4):
+            for i, c in enumerate(blocks):
                 for r, term in enumerate(terms):
                     nc.tensor.matmul(
-                        acc[:, c * P : (c + 1) * P],
+                        acc[:, i * P : (i + 1) * P],
                         term[:, c * P : (c + 1) * P],
                         ident[:],
                         start=(r == 0),
                         stop=(r == len(terms) - 1),
                         is_transpose=True,
                     )
-            return acc
+            nc.scalar.copy(out=res[:, blocks[0] * P : (blocks[-1] + 1) * P], in_=acc[:, 0 : len(blocks) * P])
 
-        for i, (nb, h) in enumerate(((0, 0), (0, 1), (1, 0))):
-            acc = sum_back([scaled_turned(nb, h, r) for r in range(TOP)], 4 + i % 2)
-            res = keep.tile([P, HALF], F32, name="res%d%d" % (nb, h))
-            nc.scalar.copy(out=res[:], in_=acc[:])
-            nc.scalar.dma_start(out=out[nb * P : (nb + 1) * P, h * HALF : (h + 1) * HALF], in_=res[:])
-        for q in range(2):
-            t0 = HALF + q * 256
+        def store(nb, t0, width, res):
+            nc.scalar.dma_start(out=out[nb * P : (nb + 1) * P, t0 : t0 + width], in_=res)
+
+        res = [keep.tile([P, HALF], F32, name="res%d" % i) for i in range(3)]
+        terms_a = [scaled_turned(0, 0, r, (7, 6, 2)[r]) for r in range(TOP)]
+        terms_b = [scaled_turned(0, 1, 0, 7)]
+        for c, nbank in enumerate((1, 5, 3, 4)):
+            sum_back(terms_a, nbank, [c], res[0])
+        store(0, 0, HALF, res[0][:])
+        terms_b.extend([scaled_turned(0, 1, r, nbank) for r, nbank in ((1, 1), (2, 5))])
+        terms_c = [scaled_turned(1, 0, r, (3, 4, 1)[r]) for r in range(TOP)]
+        sum_back(terms_b, 7, [0, 1, 2, 3], res[1])
+        store(0, HALF, HALF, res[1][:])
+        for c, nbank in ((0, 6), (2, 2)):
+            sum_back(terms_c, nbank, [c, c + 1], res[2])
+            store(1, c * P, 2 * P, res[2][:, c * P : (c + 2) * P])
+        for q, (c0, width) in enumerate(((0, 384), (384, 128))):
+            t0 = HALF + c0
             terms = []
             for r in range(TOP):
-                z = keep.tile([P, 256], F32, name="term%d%d" % (q, r))
+                z = keep.tile([P, width], F32, name="term%d%d" % (q, r))
                 nc.vector.tensor_tensor(
-                    z[:], y[1][:].indirect(pos_t[r][:, t0 // 16 : (t0 + 256) // 16]), gate_last[:, r, q * 256 : (q + 1) * 256], ALU.mult
+                    z[:], y[1][:].indirect(pos_t[r][:, t0 // 16 : (t0 + width) // 16]), gate_last[:, r, c0 : c0 + width], ALU.mult
                 )
                 terms.append(z)
-            part = keep.tile([P, 256], F32, name="part%d" % q)
+            part = keep.tile([P, width], F32, name="part%d" % q)
             nc.vector.tensor_tensor(part[:], terms[0][:], terms[1][:], ALU.add)
-            res = keep.tile([P, 256], F32, name="last%d" % q)
-            nc.vector.tensor_tensor(res[:], part[:], terms[2][:], ALU.add)
-            nc.sync.dma_start(out=out[P : 2 * P, t0 : t0 + 256], in_=res[:])
+            total = keep.tile([P, width], F32, name="total%d" % q)
+            nc.vector.tensor_tensor(total[:], part[:], terms[2][:], ALU.add)
+            nc.sync.dma_start(out=out[P : 2 * P, t0 : t0 + width], in_=total[:])

@@ -100,7 +100,7 @@ def tile_moe_prv_lin_relu_kernel(
             return quantize(grouped[:], K, "wu_q%d" % g)
 
         def cast_u(raw, c0, width, on_vector, name):
-            grouped = keep.tile([P, 4 * width], BF16, name=name + "_bf", align_bytes=64)
+            grouped = keep.tile([P, 4 * width], BF16, name=name + "_bf", tag=name + "_bf", align_bytes=64)
             dst = grouped[:].rearrange("p (c i j) -> p c j i", i=4, j=4)
             src = raw[:, :, c0 : c0 + width].rearrange("p j (c i) -> p c j i", i=4)
             if on_vector:
@@ -152,17 +152,17 @@ def tile_moe_prv_lin_relu_kernel(
         bf_b = cast_u(u0_raw[1], 256, 256, False, "u0d")
         x_pairs = [
             keep.tile([P, T], U32, name="x_pairs0", tag="u0_raw1"),
-            keep.tile([P, T], U32, name="x_pairs1"),
-        ]
+            ]
         project(0, 0, False, 0)
         project(1, 0, False, 2)
-        project(0, 1, False, 1)
-        project(1, 1, False, 3)
         u0_q[2] = quantize(bf_a, 256, "u0_q2")
         bf_a = cast_u(u1_raw[2], 0, 256, True, "u1c")
         u0_q[3] = quantize(bf_b, 256, "u0_q3")
-        bf_b = cast_u(u1_raw[3], 0, 128, True, "u1d")
+        x_pairs.append(keep.tile([P, T], U32, name="x_pairs1", tag="u0d_bf", align_bytes=64))
+        project(0, 1, False, 1)
+        project(1, 1, False, 3)
         u1_q[2] = quantize(bf_a, 256, "u1_q2")
+        bf_b = cast_u(u1_raw[3], 0, 128, True, "u1d")
         bf_a = cast_u(u1_raw[4], 0, 128, True, "u1e")
         u1_q[3] = quantize(bf_b, 128, "u1_q3")
         u1_q[4] = quantize(bf_a, 128, "u1_q4")
@@ -190,38 +190,41 @@ def tile_moe_prv_lin_relu_kernel(
                 in_=stage[n % 3][:, cols].rearrange("p (u s) -> p s u", u=2),
             )
 
-        def quantize_slots(n, name):
+        def quantize_slots(n, name, piece):
+            s0, width = SLOT_CHUNKS[n]
             woven = stage[(n + 2) % 3]
             return [
-                quantize(woven[:, 2 * C * i : 2 * C * (i + 1)].bitcast(BF16), C, name + str(i))
-                for i in range(SLOT_CHUNKS[n][1] // C)
+                (s0 + c0, piece) + quantize(woven[:, 2 * c0 : 2 * (c0 + piece)].bitcast(BF16), piece, name + str(c0))
+                for c0 in range(0, width, piece)
             ]
 
-        def multiply(n, xq, nb, nbank):
-            s0, width = SLOT_CHUNKS[n]
+        def multiply(pieces, nb, nbank):
             acc = bank(nbank)
-            for i in range(width // C):
-                e = s0 // C + i
+            for s0, width, codes, scales in pieces:
+                e = s0 // C
+                c0 = s0 - pieces[0][0]
                 nc.tensor.matmul_mx(
-                    out=acc[:, i * C : (i + 1) * C],
+                    out=acc[:, c0 : c0 + width],
                     lhsT=w_codes[e // 4][:, e % 4, nb * 4 * P : (nb + 1) * 4 * P].bitcast(FP8X4),
                     lhsT_scale=w_planes[:, e, nb * P : (nb + 1) * P],
-                    rhs=xq[i][0][:].bitcast(FP8X4),
-                    rhs_scale=xq[i][1][:],
+                    rhs=codes[:].bitcast(FP8X4),
+                    rhs_scale=scales[:],
                     start=True,
                     stop=True,
                 )
-            return acc
+            return acc, nb, pieces[0][0], sum(piece[1] for piece in pieces)
 
-        def bias_relu(n, nb, acc, on_vector):
-            s0, width = SLOT_CHUNKS[n]
-            for i in range(width // C):
-                e = s0 // C + i
-                dst = y[nb][:, e * C : (e + 1) * C]
+        def bias_relu(product, on_vector):
+            acc, nb, s0, width = product
+            for c0 in range(0, width, C):
+                e = (s0 + c0) // C
+                cols = min(C, width - c0)
+                src = acc[:, c0 : c0 + cols]
+                dst = y[nb][:, s0 + c0 : s0 + c0 + cols]
                 if on_vector:
-                    nc.vector.tensor_scalar(dst, acc[:, i * C : (i + 1) * C], bias[:, nb, e : e + 1], 0.0, ALU.add, ALU.max)
+                    nc.vector.tensor_scalar(dst, src, bias[:, nb, e : e + 1], 0.0, ALU.add, ALU.max)
                 else:
-                    nc.scalar.activation(out=dst, in_=acc[:, i * C : (i + 1) * C], func=ACT.Relu, bias=bias[:, nb, e : e + 1])
+                    nc.scalar.activation(out=dst, in_=src, func=ACT.Relu, bias=bias[:, nb, e : e + 1])
 
         gate_cols = keep.tile([P, TOP, 8], F32, name="gate_cols")
 
@@ -235,29 +238,32 @@ def tile_moe_prv_lin_relu_kernel(
         gather(1, 0, 512)
         weave(0, 0, 256)
         for n in range(4):
-            xq = quantize_slots(n, "xq")
+            xq = quantize_slots(n, "xq", C)
             weave(n + 1, 0, 512)
             gather(n + 2, 0, 512)
             for nb in range(2):
-                bias_relu(n, nb, multiply(n, xq, nb, 2 + 2 * (n % 2) + nb), False)
+                bias_relu(multiply(xq, nb, 2 + 2 * (n % 2) + nb), False)
             if n == 1:
                 turn_gate()
-        xq = quantize_slots(4, "xq")
+        xq = quantize_slots(4, "xq", C)
         weave(5, 0, 512)
         gather(6, 0, 128)
         gather(6, 128, 128)
         weave(6, 0, 128)
         weave(6, 128, 128)
-        first_rows = multiply(4, xq, 0, 2)
-        late = [(4, multiply(4, xq, 1, 3))]
-        bias_relu(4, 0, first_rows, False)
-        tail = [quantize_slots(5, "xq5_"), quantize_slots(6, "xq6_")]
-        for n, nbank in ((5, 4), (6, 6)):
-            bias_relu(n, 0, multiply(n, tail[n - 5], 0, nbank), n == 6)
-        for n, nbank in ((5, 6), (6, 0)):
-            late.append((n, multiply(n, tail[n - 5], 1, nbank)))
-        for n, acc in late:
-            bias_relu(n, 1, acc, False)
+        first_rows = multiply(xq, 0, 2)
+        late = [multiply(xq, 1, 3)]
+        bias_relu(first_rows, False)
+        xq5 = quantize_slots(5, "xq5_", C)
+        xq6 = quantize_slots(6, "xq6_", P)
+        for piece, nbank in zip(xq5, (4, 5)):
+            bias_relu(multiply([piece], 0, nbank), False)
+        for piece, nbank in zip(xq6, (6, 7)):
+            bias_relu(multiply([piece], 0, nbank), True)
+        late.append(multiply(xq5, 1, 7))
+        late.append(multiply(xq6, 1, 5))
+        for product in late:
+            bias_relu(product, False)
 
         def scaled_turned(nb, h, r, nbank):
             got = keep.tile([P, HALF], F32, name="got%d%d%d" % (nb, h, r))
@@ -293,16 +299,16 @@ def tile_moe_prv_lin_relu_kernel(
             nc.scalar.dma_start(out=out[nb * P : (nb + 1) * P, t0 : t0 + width], in_=res)
 
         res = [keep.tile([P, HALF], F32, name="res%d" % i) for i in range(3)]
-        terms_a = [scaled_turned(0, 0, r, (7, 6, 2)[r]) for r in range(TOP)]
-        terms_b = [scaled_turned(0, 1, 0, 7)]
+        terms_a = [scaled_turned(0, 0, r, (6, 7, 2)[r]) for r in range(TOP)]
+        terms_b = [scaled_turned(0, 1, 0, 6)]
         for c, nbank in enumerate((1, 5, 3, 4)):
             sum_back(terms_a, nbank, [c], res[0])
         store(0, 0, HALF, res[0][:])
         terms_b.extend([scaled_turned(0, 1, r, nbank) for r, nbank in ((1, 1), (2, 5))])
         terms_c = [scaled_turned(1, 0, r, (3, 4, 1)[r]) for r in range(TOP)]
-        sum_back(terms_b, 7, [0, 1, 2, 3], res[1])
+        sum_back(terms_b, 6, [0, 1, 2, 3], res[1])
         store(0, HALF, HALF, res[1][:])
-        for c, nbank in ((0, 6), (2, 2)):
+        for c, nbank in ((0, 7), (2, 2)):
             sum_back(terms_c, nbank, [c, c + 1], res[2])
             store(1, c * P, 2 * P, res[2][:, c * P : (c + 2) * P])
         for q, (c0, width) in enumerate(((0, 384), (384, 128))):

from contextlib import ExitStack

import concourse.mybir as mybir
from concourse.masks import make_identity

F32 = mybir.dt.float32
BF16 = mybir.dt.bfloat16
I32 = mybir.dt.int32
U32 = mybir.dt.uint32
U16 = mybir.dt.uint16
U8 = mybir.dt.uint8
FP8X4 = mybir.dt.float8_e4m3fn_x4
ACT = mybir.ActivationFunctionType
ALU = mybir.AluOpType

P = 128
F, K, T, E, C, N, TOP = 1024, 512, 1024, 12, 256, 256, 3
S = E * C
HALF = T // 2
FLOPS = 2 * F * K * T + 2 * K * N * S
BYTES = 4 * F * T + 4 * F * K + E * K * N + E * 16 * N + 4 * N * E + 4 * TOP * T + 2 * P * (S + TOP * T) // 16 + 4 * N * T

TOKEN_PIECES = [(0, 256), (256, 256), (512, 256), (768, 128), (896, 128)]
SLOT_CHUNKS = [(0, 256), (256, 512), (768, 512), (1280, 512), (1792, 512), (2304, 512), (2816, 256)]


def tile_moe_prv_lin_relu_kernel(
    tc, uT, wu, w_words, w_scales, b, gate, offs, pos1, pos2, pos3, out
):
    nc = tc.nc
    with ExitStack() as ctx:
        keep = ctx.enter_context(tc.tile_pool(name="keep", bufs=1))
        psum = ctx.enter_context(tc.psum_pool(name="psum", bufs=1))

        def bank(i):
            return psum.tile([P, 512], F32, name="bank%d" % i, tag="bank%d" % i)

        def load_rows(src, g, c0, width, name):
            raw = keep.tile([P, 4, width], F32, name=name, tag=name)
            nc.sync.dma_start(out=raw[:], in_=src[g * 512 : (g + 1) * 512, c0 : c0 + width].rearrange("(p j) w -> p j w", j=4))
            return raw

        w_planes = keep.tile([P, E, N], U8, name="w_planes", align_bytes=64)
        nc.vector.memset(w_planes[:].bitcast(I32), 0)
        gate_rows = keep.tile([P, TOP, P], F32, name="gate_rows")
        nc.vector.memset(gate_rows[:], 0.0)
        ident = keep.tile([P, P], F32, name="ident")
        make_identity(nc, ident[:])

        wu_raw = [None, None]
        u0_raw = [None, None]
        u1_raw = [None] * len(TOKEN_PIECES)
        wu_raw[0] = load_rows(wu, 0, 0, K, "wu_raw0")
        u0_raw[0] = load_rows(uT, 0, 0, HALF, "u0_raw0")
        wu_raw[1] = load_rows(wu, 1, 0, K, "wu_raw1")
        u1_raw[0] = load_rows(uT, 1, 0, HALF, "u1_raw0")
        u0_raw[1] = load_rows(uT, 0, HALF, HALF, "u0_raw1")
        for i in range(2, len(TOKEN_PIECES)):
            u1_raw[i] = load_rows(uT, 1, *TOKEN_PIECES[i], "u1_raw%d" % i)

        offs_t = keep.tile([P, S // 16], U16, name="offs_t")
        nc.sync.dma_start(offs_t[:], offs)
        for r in range(4):
            nc.sync.dma_start(
                out=w_planes[r:P:32, :, :].bitcast(I32),
                in_=w_scales[:, 0, r:16:4, :].rearrange("e q n -> q e n").bitcast(I32),
            )
        bias = keep.tile([P, 2, E], F32, name="bias")
        nc.sync.dma_start(out=bias[:], in_=b.rearrange("(c p) e -> p c e", p=P))
        w_codes = []
        for i in range(3):
            wt = keep.tile([P, 4, 4 * N], U8, name="w_codes%d" % i, align_bytes=64)
            nc.sync.dma_start(
                out=wt[:].bitcast(I32),
                in_=w_words[4 * i : 4 * i + 4, 0].rearrange("e p n r -> p e (n r)").bitcast(I32),
            )
            w_codes.append(wt)
        nc.sync.dma_start(out=gate_rows[0:8, :, :], in_=gate[:, 0, :].rearrange("r (c t) -> c r t", t=P))
        pos_t = []
        for i, pos in enumerate((pos1, pos2, pos3)):
            pt = keep.tile([P, T // 16], U16, name="pos_t%d" % i)
            nc.sync.dma_start(pt[:], pos)
            pos_t.append(pt)
        gate_last = keep.tile([P, TOP, HALF], F32, name="gate_last")
        nc.sync.dma_start(out=gate_last[:], in_=gate[:, 0:P, HALF:T].rearrange("r p t -> p r t"))

        def quantize(grouped, width, name):
            codes = keep.tile([P, width], U32, name=name + "_c", tag=name + "_c", align_bytes=64)
            scales = keep.tile([P, width], U8, name=name + "_s", tag=name + "_s", align_bytes=64)
            nc.vector.quantize_mx(out=codes[:].bitcast(FP8X4), scales=scales[:], in_=grouped)
            return codes, scales

        def prep_wu(g):
            grouped = keep.tile([P, 4 * K], BF16, name="wu_bf%d" % g, align_bytes=64)
            dst = grouped[:].rearrange("p (t m j) -> p m t j", t=4, j=4)
            src = wu_raw[g][:].rearrange("p j (m t) -> p m t j", t=4)
            cut = 80
            nc.vector.tensor_copy(out=dst[:, 0:cut], in_=src[:, 0:cut])
            nc.scalar.activation(out=dst[:, cut:P], in_=src[:, cut:P], func=ACT.Copy)
            return quantize(grouped[:], K, "wu_q%d" % g)

        def cast_u(raw, c0, width, on_vector, name):
            grouped = keep.tile([P, 4 * width], BF16, name=name + "_bf", tag=name + "_bf", align_bytes=64)
            dst = grouped[:].rearrange("p (c i j) -> p c j i", i=4, j=4)
            src = raw[:, :, c0 : c0 + width].rearrange("p j (c i) -> p c j i", i=4)
            if on_vector:
                nc.vector.tensor_copy(out=dst, in_=src)
            else:
                nc.scalar.activation(out=dst, in_=src, func=ACT.Copy)
            return grouped[:]


        def project(i, u, on_vector, nbank):
            t0, width = TOKEN_PIECES[i]
            acc = bank(nbank)
            first = u0_q[t0 // 256]
            c0 = t0 % 256
            for e in range(2):
                cols = slice((2 * u + e) * P, (2 * u + e + 1) * P)
                for g in range(2):
                    codes, scales = (first[0][:, c0 : c0 + width], first[1][:, c0 : c0 + width]) if g == 0 else (u1_q[i][0][:], u1_q[i][1][:])
                    nc.tensor.matmul_mx(
                        out=acc[:, e * width : (e + 1) * width],
                        lhsT=wu_q[g][0][:, cols].bitcast(FP8X4),
                        lhsT_scale=wu_q[g][1][:, cols],
                        rhs=codes.bitcast(FP8X4),
                        rhs_scale=scales,
                        start=(g == 0),
                        stop=(g == 1),
                    )
            dst = x_pairs[u][:, t0 : t0 + width].bitcast(BF16).rearrange("p (t e) -> p t e", e=2)
            src = acc[:, 0 : 2 * width].rearrange("p (e t) -> p t e", e=2)
            if on_vector:
                nc.vector.tensor_copy(out=dst, in_=src)
            else:
                nc.scalar.copy(out=dst, in_=src)

        wu_q = [None, None]
        u0_q = [None] * 4
        u1_q = [None] * len(TOKEN_PIECES)
        wu_q[0] = prep_wu(0)
        bf_a = cast_u(u0_raw[0], 0, 256, True, "u0a")
        bf_b = cast_u(u0_raw[0], 256, 256, False, "u0b")
        u0_q[0] = quantize(bf_a, 256, "u0_q0")
        u0_q[1] = quantize(bf_b, 256, "u0_q1")
        wu_q[1] = prep_wu(1)
        bf_a = cast_u(u1_raw[0], 0, 256, True, "u1a")
        bf_b = cast_u(u1_raw[0], 256, 256, False, "u1b")
        u1_q[0] = quantize(bf_a, 256, "u1_q0")
        u1_q[1] = quantize(bf_b, 256, "u1_q1")
        bf_a = cast_u(u0_raw[1], 0, 256, True, "u0c")
        bf_b = cast_u(u0_raw[1], 256, 256, False, "u0d")
        x_pairs = [
            keep.tile([P, T], U32, name="x_pairs0", tag="u0_raw1"),
            ]
        project(0, 0, False, 0)
        project(1, 0, False, 2)
        u0_q[2] = quantize(bf_a, 256, "u0_q2")
        bf_a = cast_u(u1_raw[2], 0, 256, True, "u1c")
        u0_q[3] = quantize(bf_b, 256, "u0_q3")
        x_pairs.append(keep.tile([P, T], U32, name="x_pairs1", tag="u0d_bf", align_bytes=64))
        project(0, 1, False, 1)
        project(1, 1, False, 3)
        u1_q[2] = quantize(bf_a, 256, "u1_q2")
        bf_b = cast_u(u1_raw[3], 0, 128, True, "u1d")
        bf_a = cast_u(u1_raw[4], 0, 128, True, "u1e")
        u1_q[3] = quantize(bf_b, 128, "u1_q3")
        u1_q[4] = quantize(bf_a, 128, "u1_q4")
        project(2, 0, False, 4)
        project(3, 0, True, 5)
        project(4, 0, True, 6)
        project(2, 1, False, 7)
        project(3, 1, False, 0)
        project(4, 1, False, 1)

        y = [keep.tile([P, S], F32, name="y%d" % nb) for nb in range(2)]
        stage = [keep.tile([P, 1024], U32, name="stage%d" % i, align_bytes=64) for i in range(3)]

        def gather(n, c0, width):
            s0 = SLOT_CHUNKS[n][0] + c0
            lst = offs_t[:, s0 // 16 : (s0 + width) // 16]
            for u in range(2):
                d0 = 2 * c0 + u * width
                nc.vector.tensor_copy(stage[n % 3][:, d0 : d0 + width], x_pairs[u][:].indirect(lst))

        def weave(n, c0, width):
            cols = slice(2 * c0, 2 * (c0 + width))
            nc.scalar.copy(
                out=stage[(n + 2) % 3][:, cols].rearrange("p (s u) -> p s u", u=2),
                in_=stage[n % 3][:, cols].rearrange("p (u s) -> p s u", u=2),
            )

        def quantize_slots(n, name, piece):
            s0, width = SLOT_CHUNKS[n]
            woven = stage[(n + 2) % 3]
            return [
                (s0 + c0, piece) + quantize(woven[:, 2 * c0 : 2 * (c0 + piece)].bitcast(BF16), piece, name + str(c0))
                for c0 in range(0, width, piece)
            ]

        def multiply(pieces, nb, nbank):
            acc = bank(nbank)
            for s0, width, codes, scales in pieces:
                e = s0 // C
                c0 = s0 - pieces[0][0]
                nc.tensor.matmul_mx(
                    out=acc[:, c0 : c0 + width],
                    lhsT=w_codes[e // 4][:, e % 4, nb * 4 * P : (nb + 1) * 4 * P].bitcast(FP8X4),
                    lhsT_scale=w_planes[:, e, nb * P : (nb + 1) * P],
                    rhs=codes[:].bitcast(FP8X4),
                    rhs_scale=scales[:],
                    start=True,
                    stop=True,
                )
            return acc, nb, pieces[0][0], sum(piece[1] for piece in pieces)

        def bias_relu(product, on_vector):
            acc, nb, s0, width = product
            for c0 in range(0, width, C):
                e = (s0 + c0) // C
                cols = min(C, width - c0)
                src = acc[:, c0 : c0 + cols]
                dst = y[nb][:, s0 + c0 : s0 + c0 + cols]
                if on_vector:
                    nc.vector.tensor_scalar(dst, src, bias[:, nb, e : e + 1], 0.0, ALU.add, ALU.max)
                else:
                    nc.scalar.activation(out=dst, in_=src, func=ACT.Relu, bias=bias[:, nb, e : e + 1])

        gate_cols = keep.tile([P, TOP, 8], F32, name="gate_cols")

        def turn_gate():
            acc = bank(6)
            for r in range(TOP):
                nc.tensor.transpose(acc[:, r * P : (r + 1) * P], gate_rows[:, r, :], ident[:])
            nc.scalar.copy(out=gate_cols[:], in_=acc[:, 0 : TOP * P].rearrange("p (r c) -> p r c", r=TOP)[:, :, 0:8])

        gather(0, 0, 256)
        gather(1, 0, 512)
        weave(0, 0, 256)
        for n in range(4):
            xq = quantize_slots(n, "xq", C)
            weave(n + 1, 0, 512)
            gather(n + 2, 0, 512)
            for nb in range(2):
                bias_relu(multiply(xq, nb, 2 + 2 * (n % 2) + nb), False)
            if n == 1:
                turn_gate()
        xq = quantize_slots(4, "xq", C)
        weave(5, 0, 512)
        gather(6, 0, 128)
        gather(6, 128, 128)
        weave(6, 0, 128)
        weave(6, 128, 128)
        first_rows = multiply(xq, 0, 2)
        late = [multiply(xq, 1, 3)]
        bias_relu(first_rows, False)
        xq5 = quantize_slots(5, "xq5_", C)
        xq6 = quantize_slots(6, "xq6_", P)
        for piece, nbank in zip(xq5, (4, 5)):
            bias_relu(multiply([piece], 0, nbank), False)
        for piece, nbank in zip(xq6, (6, 7)):
            bias_relu(multiply([piece], 0, nbank), True)
        late.append(multiply(xq5, 1, 7))
        late.append(multiply(xq6, 1, 5))
        for product in late:
            bias_relu(product, False)

        def scaled_turned(nb, h, r, nbank):
            got = keep.tile([P, HALF], F32, name="got%d%d%d" % (nb, h, r))
            nc.vector.tensor_copy(got[:], y[nb][:].indirect(pos_t[r][:, h * 32 : (h + 1) * 32]))
            acc = bank(nbank)
            for c in range(4):
                nc.tensor.transpose(acc[:, c * P : (c + 1) * P], got[:, c * P : (c + 1) * P], ident[:])
            scaled = keep.tile([P, HALF], F32, name="scaled%d%d%d" % (nb, h, r))
            for c in range(4):
                nc.scalar.activation(
                    out=scaled[:, c * P : (c + 1) * P],
                    in_=acc[:, c * P : (c + 1) * P],
                    func=ACT.Copy,
                    scale=gate_cols[:, r, 4 * h + c : 4 * h + c + 1],
                )
            return scaled

        def sum_back(terms, nbank, blocks, res):
            acc = bank(nbank)
            for i, c in enumerate(blocks):
                for r, term in enumerate(terms):
                    nc.tensor.matmul(
                        acc[:, i * P : (i + 1) * P],
                        term[:, c * P : (c + 1) * P],
                        ident[:],
                        start=(r == 0),
                        stop=(r == len(terms) - 1),
                        is_transpose=True,
                    )
            nc.scalar.copy(out=res[:, blocks[0] * P : (blocks[-1] + 1) * P], in_=acc[:, 0 : len(blocks) * P])

        def store(nb, t0, width, res):
            nc.scalar.dma_start(out=out[nb * P : (nb + 1) * P, t0 : t0 + width], in_=res)

        res = [keep.tile([P, HALF], F32, name="res%d" % i) for i in range(3)]
        terms_a = [scaled_turned(0, 0, r, (6, 7, 2)[r]) for r in range(TOP)]
        terms_b = [scaled_turned(0, 1, 0, 6)]
        for c, nbank in enumerate((1, 5, 3, 4)):
            sum_back(terms_a, nbank, [c], res[0])
        store(0, 0, HALF, res[0][:])
        terms_b.extend([scaled_turned(0, 1, r, nbank) for r, nbank in ((1, 1), (2, 5))])
        terms_c = [scaled_turned(1, 0, r, (3, 4, 1)[r]) for r in range(TOP)]
        sum_back(terms_b, 6, [0, 1, 2, 3], res[1])
        store(0, HALF, HALF, res[1][:])
        for c, nbank in ((0, 7), (2, 2)):
            sum_back(terms_c, nbank, [c, c + 1], res[2])
            store(1, c * P, 2 * P, res[2][:, c * P : (c + 2) * P])
        for q, (c0, width) in enumerate(((0, 384), (384, 128))):
            t0 = HALF + c0
            terms = []
            for r in range(TOP):
                z = keep.tile([P, width], F32, name="term%d%d" % (q, r))
                nc.vector.tensor_tensor(
                    z[:], y[1][:].indirect(pos_t[r][:, t0 // 16 : (t0 + width) // 16]), gate_last[:, r, c0 : c0 + width], ALU.mult
                )
                terms.append(z)
            part = keep.tile([P, width], F32, name="part%d" % q)
            nc.vector.tensor_tensor(part[:], terms[0][:], terms[1][:], ALU.add)
            total = keep.tile([P, width], F32, name="total%d" % q)
            nc.vector.tensor_tensor(total[:], part[:], terms[2][:], ALU.add)
            nc.sync.dma_start(out=out[P : 2 * P, t0 : t0 + width], in_=total[:])
